import numpy as np
import ml_dtypes


def mxq(x, axis, fmt="e4m3"):
    dtype, down = {"e4m3": (ml_dtypes.float8_e4m3fn, 7), "e5m2": (ml_dtypes.float8_e5m2, 14)}[fmt]
    v = np.moveaxis(np.asarray(x, np.float32).astype(ml_dtypes.bfloat16).astype(np.float64), axis, -1)
    blocks = v.reshape(v.shape[:-1] + (-1, 32))
    amax = np.abs(blocks).max(-1, keepdims=True)
    byte = np.maximum(np.where(amax > 0, np.frexp(amax)[1] - 1 + 127, 0) - down, 1)
    scale = np.exp2(byte - 127.0)
    codes = (blocks / scale).astype(np.float32).astype(dtype).astype(np.float64)
    return np.moveaxis((codes * scale).reshape(v.shape), -1, axis)


WIDE = False


def mx_kscale(k):
    if not WIDE:
        return np.ones(k)
    levels = np.array([10, -10, 5, -5, 0])
    if k % 512:
        return np.exp2(np.random.permutation(np.resize(levels, k // 32))).repeat(32)
    a = np.empty((k // 512, 16))
    for p in range(k // 512):
        a[p, :8] = np.random.permutation(np.resize(levels, 8))
        for g in range(8):
            far = levels[np.abs(levels - a[p, g]) >= 10]
            a[p, g + 8] = far[np.random.randint(len(far))]
    return np.exp2(a.ravel()).repeat(32)


def f64(x):
    return np.asarray(x).astype(np.float64)


def striped(idx):
    return np.tile(idx.reshape(-1, 16).T, (8, 1)).astype(np.uint16)


def unstriped(offs):
    return offs[:16].T.reshape(-1).astype(np.int64)


def striped8(idx):
    return np.concatenate([x.reshape(-1, 16).T for x in idx]).astype(np.uint16)


def runs(offs, k):
    lists = np.stack([offs[16 * r : 16 * r + 16].T.reshape(-1) for r in range(8)]).astype(np.int64)
    return lists[np.arange(k) % 512 // 64]


def pack_weight(w):
    k, n = w.shape
    w = f64(np.asarray(w, np.float32).astype(ml_dtypes.bfloat16)).reshape(k // 32, 32, n)
    amax = np.abs(w).max(1)
    byte = np.clip(np.where(amax > 0, np.frexp(amax)[1] - 1 + 127 - 7, 1), 1, 254)
    scaled = (w * np.exp2(127.0 - byte)[:, None, :]).reshape(k, n).astype(np.float32)
    words = np.ascontiguousarray(scaled.reshape(k // 512, 128, 4, n).transpose(0, 1, 3, 2)).astype(ml_dtypes.float8_e4m3fn).view(np.uint8)
    return words, np.ascontiguousarray(byte.astype(np.uint8).reshape(k // 512, 16, n))


def unpack_weight(words, scales):
    g, p, n, _ = words.shape
    vals = np.ascontiguousarray(words).view(ml_dtypes.float8_e4m3fn).astype(np.float64) * np.repeat(np.exp2(scales.astype(np.float64) - 127.0), 8, axis=1)[..., None]
    return vals.transpose(0, 1, 3, 2).reshape(g * 512, n)


E2M1 = np.array([0.0, 0.5, 1.0, 1.5, 2.0, 3.0, 4.0, 6.0, -0.0, -0.5, -1.0, -1.5, -2.0, -3.0, -4.0, -6.0])


def pack_fp4(w):
    k, n = w.shape
    w = f64(np.asarray(w, np.float32).astype(ml_dtypes.bfloat16)).reshape(k // 32, 32, n)
    amax = np.abs(w).max(1)
    mant, ex = np.frexp(amax / 6.0)
    byte = np.clip(np.where(amax > 0, np.where(mant > 0.5, ex, ex - 1) + 127, 1), 1, 254)
    scaled = (w * np.exp2(127.0 - byte)[:, None, :]).reshape(k, n).astype(np.float32)
    c = np.ascontiguousarray(scaled.reshape(k // 512, 128, 4, n).transpose(0, 1, 3, 2)).astype(ml_dtypes.float4_e2m1fn).view(np.uint8) & 0xF
    words = (c[..., 0::2] | (c[..., 1::2] << 4)).reshape(k // 512, 128, 2 * n)
    return np.ascontiguousarray(words), np.ascontiguousarray(byte.astype(np.uint8).reshape(k // 512, 16, n))


def unpack_fp4(words, scales):
    g, _, n = scales.shape
    words = np.ascontiguousarray(words).reshape(g, 128, n, 2)
    nib = np.empty((g, 128, n, 4), np.uint8)
    nib[..., 0::2] = words & 0xF
    nib[..., 1::2] = words >> 4
    vals = E2M1[nib] * np.repeat(np.exp2(scales.astype(np.float64) - 127.0), 8, axis=1)[..., None]
    return vals.transpose(0, 1, 3, 2).reshape(g * 512, n)


def planes(y):
    n, m = y.shape
    v = y.astype(np.float32).astype(ml_dtypes.bfloat16).astype(np.float64).reshape(n // 32, 32, m)
    top = np.abs(v).max(1)
    byte = np.clip(np.where(top > 0, np.frexp(top)[1] - 1 + 127 - 7, 1), 1, 254)
    codes = (v * np.exp2(127.0 - byte)[:, None, :]).reshape(n, m).astype(np.float32).astype(ml_dtypes.float8_e4m3fn).view(np.uint8)
    words = codes.reshape(n // 512, 128, 4, m).transpose(0, 1, 3, 2)
    return np.ascontiguousarray(words), np.ascontiguousarray(byte.astype(np.uint8).reshape(n // 512, 16, m))


K, T, S, N, G, H = 512, 1024, 256, 512, 2048, 512


def setup_inputs():
    n = np.random.standard_normal
    s = mx_kscale(K)[:, None]
    u = mx_kscale(K)
    packed_xT = pack_weight(n((K, T)) * s)
    packed_dT = pack_weight(n((K, G)) / s)
    packed_w1 = pack_fp4(n((H, N)) / np.sqrt(H) / u[:, None])
    return {
        "x_words": packed_xT[0],
        "x_scales": packed_xT[1],
        "d_words": packed_dT[0],
        "d_scales": packed_dT[1],
        "gn": (np.random.uniform(0.5, 1.5, (H, 1)) * u[:, None]).astype(np.float32),
        "w1_words": packed_w1[0],
        "w1_scales": packed_w1[1],
        "offs": striped(np.random.permutation(T)[:S]),
        "k1": striped8(np.random.randint(0, G, (8, H))),
        "two": striped(np.random.permutation(T)[:S]),
        "k2": striped8(np.random.randint(0, G, (8, H))),
        "n1": striped(np.random.permutation(S)),
        "n2": striped(np.random.permutation(S)),
        "n3": striped8(np.stack([np.random.permutation(S) for _ in range(8)])),
        "n4": striped8(np.stack([np.random.permutation(S) for _ in range(8)])),
        "n5": striped8(np.stack([np.random.permutation(S) for _ in range(8)])),
    }


def reference(x_words, x_scales, d_words, d_scales, gn, w1_words, w1_scales, offs, k1, two, k2, n1, n2, n3, n4, n5):
    d_k1 = unpack_weight(d_words, d_scales)[np.arange(K)[:, None], runs(k1, K)]
    xq = unpack_weight(x_words, x_scales)[:, unstriped(offs)]
    a = 0.0625 * (d_k1.T @ xq)
    d_k2 = unpack_weight(d_words, d_scales)[np.arange(K)[:, None], runs(k2, K)]
    x_two = unpack_weight(x_words, x_scales)[:, unstriped(two)]
    b = 0.0625 * (d_k2.T @ x_two)
    z = f64(gn) * (a[:, unstriped(n1)] - (np.tanh(b) * b[:, unstriped(n2)]))
    h = unpack_fp4(w1_words, w1_scales).T @ mxq(z, 0, "e4m3")
    out_0 = 0.75 * (h * (h[np.arange(N)[:, None], runs(n3, N)]) + (h[np.arange(N)[:, None], runs(n4, N)]) * (h[np.arange(N)[:, None], runs(n5, N)]))
    return (out_0,) + planes(out_0)

@@ -1,0 +1,199 @@
+from contextlib import ExitStack
+
+import concourse.mybir as mybir
+
+K, T, S, N, G, H = 512, 1024, 256, 512, 2048, 512
+FLOPS = 2 * K * H * S * 2 + 2 * H * N * S
+
+F32 = mybir.dt.float32
+BF16 = mybir.dt.bfloat16
+I32 = mybir.dt.int32
+U32 = mybir.dt.uint32
+U16 = mybir.dt.uint16
+U8 = mybir.dt.uint8
+FP8X4 = mybir.dt.float8_e4m3fn_x4
+FP4X4 = mybir.dt.float4_e2m1fn_x4
+MULT = mybir.AluOpType.mult
+ADD = mybir.AluOpType.add
+SUB = mybir.AluOpType.subtract
+COPY = mybir.ActivationFunctionType.Copy
+TANH = mybir.ActivationFunctionType.Tanh
+
+P = 128
+PACK = 4
+HALF = S // 2
+
+
+def tile_picked_twpqsoftbdot_none_po_kernel(
+    tc, x_words, x_scales, d_words, d_scales, gn, w1_words, w1_scales, offs, k1, two, k2, n1, n2, n3, n4, n5, out_0, out_1, out_2
+):
+    nc = tc.nc
+    with ExitStack() as ctx:
+        sb = ctx.enter_context(tc.tile_pool(name="sb", bufs=1))
+        ps = ctx.enter_context(tc.psum_pool(name="ps", bufs=1))
+
+        def load_list(name, src):
+            tile = sb.tile(list(src.shape), U16, name=name)
+            nc.sync.dma_start(tile[:], src)
+            return tile
+
+        def load_scale_rows(name, src, width):
+            tile = sb.tile([P, width], U8, name=name, align_bytes=64)
+            nc.sync.dma_start(tile[:].bitcast(I32), src[0].bitcast(I32).unsqueeze(1).to_broadcast([16, 8, width // 4]))
+            return tile
+
+        k2_t = load_list("k2_t", k2)
+        d_sc = load_scale_rows("d_sc", d_scales, G)
+        two_t = load_list("two_t", two)
+        x_sc = load_scale_rows("x_sc", x_scales, T)
+        d_w = sb.tile([P, G], U32, name="d_w", align_bytes=64)
+        nc.sync.dma_start(d_w[:].bitcast(I32), d_words[0].rearrange("p c r -> p (c r)").bitcast(I32))
+        x_w = sb.tile([P, T], U32, name="x_w", align_bytes=64)
+        nc.sync.dma_start(x_w[:].bitcast(I32), x_words[0].rearrange("p c r -> p (c r)").bitcast(I32))
+        k1_t = load_list("k1_t", k1)
+        offs_t = load_list("offs_t", offs)
+        n2_t = load_list("n2_t", n2)
+        n1_t = load_list("n1_t", n1)
+        n3_t = load_list("n3_t", n3)
+        gn_t = sb.tile([P, PACK], F32, name="gn_t", tag="slot_g")
+        nc.sync.dma_start(gn_t[:], gn.rearrange("(p t) o -> p (t o)", t=PACK))
+        w_sc = load_scale_rows("w_sc", w1_scales, N)
+        n4_t = load_list("n4_t", n4)
+        n5_t = load_list("n5_t", n5)
+        w_w = sb.tile([P, 2 * N], U8, name="w_w", align_bytes=64)
+        nc.sync.dma_start(w_w[:].bitcast(I32), w1_words[0].bitcast(I32))
+
+        def deal_bytes(dst, src):
+            nc.vector.tensor_copy(dst.rearrange("p (t g i) -> p g t i", t=PACK, i=16), src.rearrange("p (g i t) -> p g t i", t=PACK, i=16))
+
+        def pick_scales(name, k_t, tok_t, extra, tag):
+            got = sb.tile([P, H + S], U8, name=name + "_got", tag=tag, align_bytes=64)
+            rows = sb.tile([P, H + S + extra], U8, name=name + "_rows", align_bytes=64)
+            nc.vector.tensor_copy(got[:, 0:H], d_sc[:].indirect(k_t[:]))
+            nc.vector.tensor_copy(got[:, H:], x_sc[:].indirect(tok_t[:]))
+            deal_bytes(rows[:, 0:H], got[:, 0:H])
+            nc.vector.tensor_copy(rows[:, H : H + S].bitcast(I32), got[:, H:].bitcast(I32))
+            return rows
+
+        def place_rows(name, rows, queue):
+            plane = sb.tile(list(rows.shape), U8, name=name + "_placed", align_bytes=64)
+            nc.gpsimd.memset(plane[:].bitcast(I32), 0)
+            for q in range(4):
+                queue.dma_start(plane[32 * q : 32 * q + 4, :].bitcast(I32), rows[32 * q : 32 * q + 32 : 8, :].bitcast(I32))
+            return plane
+
+        def pick_words(name, k_t, tok_t, x_tag, d_tag, dealt_tag):
+            x_got = sb.tile([P, S], U32, name=name + "_xw", tag=x_tag, align_bytes=64)
+            d_got = sb.tile([P, H], U32, name=name + "_dw", tag=d_tag, align_bytes=64)
+            dealt = sb.tile([P, H], U32, name=name + "_dealt", tag=dealt_tag, align_bytes=64)
+            nc.vector.tensor_copy(d_got[:], d_w[:].indirect(k_t[:]))
+            nc.vector.tensor_copy(x_got[:], x_w[:].indirect(tok_t[:]))
+            nc.vector.tensor_copy(dealt[:].rearrange("p (t g i) -> p g t i", t=PACK, i=4), d_got[:].rearrange("p (g i t) -> p g t i", t=PACK, i=4))
+            return dealt, x_got
+
+        def product(bank_name, dealt, x_got, plane):
+            banks = []
+            for t in range(PACK):
+                bank = ps.tile([P, S], F32, name=bank_name + str(t))
+                cols = slice(t * P, (t + 1) * P)
+                nc.tensor.matmul_mx(
+                    bank[:],
+                    lhsT=dealt[:, cols].bitcast(FP8X4),
+                    lhsT_scale=plane[:, cols],
+                    rhs=x_got[:].bitcast(FP8X4),
+                    rhs_scale=plane[:, H : H + S],
+                    start=True,
+                    stop=True,
+                )
+                banks.append(bank)
+            return banks
+
+        plane_b = place_rows("b", pick_scales("b", k2_t, two_t, 0, "b_got"), nc.scalar)
+        dealt_b, xw_b = pick_words("b", k2_t, two_t, "slot_y", "slot_x", "slot_z")
+        bank_b = product("acc_b", dealt_b, xw_b, plane_b)
+        b_win = [sb.tile([P, 2 * S], F32, name="b_win" + str(t)) for t in range(PACK)]
+        h_win = [sb.tile([P, 2 * S], F32, name="h_win" + str(t)) for t in range(PACK)]
+        for t in range(PACK):
+            nc.scalar.activation(b_win[t][:, S:], bank_b[t][:], TANH, scale=0.0625)
+            nc.scalar.activation(b_win[t][:, :S], bank_b[t][:], COPY, scale=gn_t[:, t : t + 1])
+        for t in range(PACK):
+            nc.scalar.activation(h_win[t][:, S:], b_win[t][:].indirect(n2_t[:]), COPY)
+
+        rows_a = pick_scales("a", k1_t, offs_t, N, "slot_x")
+        deal_bytes(rows_a[:, H + S :], w_sc[:])
+        plane_a = place_rows("a", rows_a, nc.sync)
+        dealt_a, xw_a = pick_words("a", k1_t, offs_t, "slot_z", "slot_y", "a_dealt")
+        bank_a = product("acc_a", dealt_a, xw_a, plane_a)
+        w_dealt = sb.tile([P, 2 * N], U8, name="w_dealt", tag="slot_y", align_bytes=64)
+        nc.vector.tensor_copy(
+            w_dealt[:].rearrange("p (t g i b) -> p g t i b", t=PACK, i=8, b=2), w_w[:].rearrange("p (g i t b) -> p g t i b", t=PACK, i=8, b=2)
+        )
+        a_win = [sb.tile([P, S], F32, name="a_win" + str(t)) for t in range(PACK)]
+        for t in range(PACK):
+            nc.vector.tensor_scalar(a_win[t][:], bank_a[t][:], gn_t[:, t : t + 1], 0.0625, MULT, MULT)
+        prod = sb.tile([P, PACK, S], F32, name="prod", tag="slot_g")
+        for t in range(PACK):
+            nc.vector.scalar_tensor_tensor(prod[:, t, :], h_win[t][:, S:], 0.0625, b_win[t][:, S:], MULT, MULT)
+
+        bank_h = [ps.tile([P, S], F32, name="acc_b" + str(t)) for t in range(PACK)]
+        for u in range(2):
+            cols = slice(u * HALF, (u + 1) * HALF)
+            ents = slice(u * HALF // 16, (u + 1) * HALF // 16)
+            a_got = sb.tile([P, PACK, HALF], F32, name="a_got" + str(u))
+            for t in range(PACK):
+                nc.scalar.activation(a_got[:, t, :], a_win[t][:].indirect(n1_t[:, ents]), COPY)
+            z_bf = sb.tile([P, HALF, PACK], BF16, name="z_bf" + str(u), align_bytes=64)
+            nc.vector.tensor_tensor(
+                z_bf[:].rearrange("p (c i) t -> p c t i", i=4),
+                a_got[:].rearrange("p t (c i) -> p c t i", i=4),
+                prod[:, :, cols].rearrange("p t (c i) -> p c t i", i=4),
+                SUB,
+            )
+            z_w = sb.tile([P, HALF], U32, name="z_w" + str(u), align_bytes=64)
+            z_sc = sb.tile([P, HALF], U8, name="z_sc" + str(u), align_bytes=64)
+            nc.vector.quantize_mx(z_w[:].bitcast(FP8X4), z_sc[:], z_bf[:].rearrange("p c t -> p (c t)"))
+            for t in range(PACK):
+                nc.tensor.matmul_mx(
+                    bank_h[t][:, cols],
+                    lhsT=w_dealt[:, 2 * t * P : 2 * (t + 1) * P].bitcast(FP4X4),
+                    lhsT_scale=plane_a[:, H + S + t * P : H + S + (t + 1) * P],
+                    rhs=z_w[:].bitcast(FP8X4),
+                    rhs_scale=z_sc[:],
+                    start=True,
+                    stop=True,
+                )
+
+        for t in range(PACK):
+            nc.vector.tensor_copy(h_win[t][:, :S], bank_h[t][:])
+
+        y = sb.tile([P, PACK, S], F32, name="y")
+        y_w = sb.tile([P, S], U32, name="y_w", align_bytes=64)
+        y_sc = sb.tile([P, S], U8, name="y_sc", align_bytes=64)
+        out_rows = out_0.rearrange("(p t) j -> p t j", t=PACK)
+        out_words = out_1[0].rearrange("p c r -> p (c r)").bitcast(I32)
+
+        def finish(t, lo, hi):
+            tag = str(t) + "_" + str(lo)
+            ents = slice(lo // 16, hi // 16)
+            got = [sb.tile([P, hi - lo], F32, name="got" + str(i) + "_" + tag) for i in range(3)]
+            for i, lst in enumerate((n3_t, n4_t, n5_t)):
+                nc.scalar.activation(got[i][:], h_win[t][:].indirect(lst[:, ents]), COPY)
+            left = sb.tile([P, hi - lo], F32, name="left" + tag)
+            right = sb.tile([P, hi - lo], F32, name="right" + tag)
+            nc.vector.scalar_tensor_tensor(left[:], h_win[t][:, lo:hi], 0.75, got[0][:], MULT, MULT)
+            nc.vector.scalar_tensor_tensor(right[:], got[1][:], 0.75, got[2][:], MULT, MULT)
+            nc.vector.tensor_tensor(y[:, t, lo:hi], left[:], right[:], ADD)
+            nc.sync.dma_start(out_rows[:, t, lo:hi], y[:, t, lo:hi])
+
+        for t in range(PACK - 1):
+            finish(t, 0, S)
+        for u in range(2):
+            lo, hi = u * HALF, (u + 1) * HALF
+            finish(PACK - 1, lo, hi)
+            y_bf = sb.tile([P, HALF, PACK], BF16, name="y_bf" + str(u), align_bytes=64)
+            nc.vector.tensor_copy(y_bf[:].rearrange("p (c i) t -> p c t i", i=4), y[:, :, lo:hi].rearrange("p t (c i) -> p c t i", i=4))
+            nc.vector.quantize_mx(y_w[:, lo:hi].bitcast(FP8X4), y_sc[:, lo:hi], y_bf[:].rearrange("p c t -> p (c t)"))
+            nc.sync.dma_start(out_words[:, lo:hi], y_w[:, lo:hi].bitcast(I32))
+        for q in range(4):
+            queue = nc.scalar if q % 2 == 0 else nc.sync
+            queue.dma_start(out_2[0, 4 * q : 4 * q + 4, :].bitcast(I32), y_sc[32 * q : 32 * q + 4, :].bitcast(I32))

@@ -37,42 +37,43 @@ def tile_picked_twpqsoftbdot_none_po_kernel(
             nc.sync.dma_start(tile[:], src)
             return tile
 
-        def load_scale_rows(name, src, width):
+        def load_scale_rows(name, src, width, queue):
             tile = sb.tile([P, width], U8, name=name, align_bytes=64)
-            nc.sync.dma_start(tile[:].bitcast(I32), src[0].bitcast(I32).unsqueeze(1).to_broadcast([16, 8, width // 4]))
+            queue.dma_start(tile[:].bitcast(I32), src[0].bitcast(I32).unsqueeze(1).to_broadcast([16, 8, width // 4]))
             return tile
 
-        k2_t = load_list("k2_t", k2)
-        d_sc = load_scale_rows("d_sc", d_scales, G)
         two_t = load_list("two_t", two)
-        x_sc = load_scale_rows("x_sc", x_scales, T)
-        d_w = sb.tile([P, G], U32, name="d_w", align_bytes=64)
-        nc.sync.dma_start(d_w[:].bitcast(I32), d_words[0].rearrange("p c r -> p (c r)").bitcast(I32))
-        x_w = sb.tile([P, T], U32, name="x_w", align_bytes=64)
-        nc.sync.dma_start(x_w[:].bitcast(I32), x_words[0].rearrange("p c r -> p (c r)").bitcast(I32))
+        x_sc = load_scale_rows("x_sc", x_scales, T, nc.scalar)
+        k2_t = load_list("k2_t", k2)
+        d_sc = load_scale_rows("d_sc", d_scales, G, nc.scalar)
         k1_t = load_list("k1_t", k1)
-        offs_t = load_list("offs_t", offs)
+        x_w = sb.tile([P, T], U32, name="x_w", align_bytes=64)
+        nc.scalar.dma_start(x_w[:].bitcast(I32), x_words[0].rearrange("p c r -> p (c r)").bitcast(I32))
         n2_t = load_list("n2_t", n2)
         n1_t = load_list("n1_t", n1)
+        d_w = sb.tile([P, G], U32, name="d_w", align_bytes=64)
+        nc.scalar.dma_start(d_w[:].bitcast(I32), d_words[0].rearrange("p c r -> p (c r)").bitcast(I32))
+        offs_t = load_list("offs_t", offs)
         n3_t = load_list("n3_t", n3)
-        gn_t = sb.tile([P, PACK], F32, name="gn_t", tag="slot_g")
-        nc.sync.dma_start(gn_t[:], gn.rearrange("(p t) o -> p (t o)", t=PACK))
-        w_sc = load_scale_rows("w_sc", w1_scales, N)
         n4_t = load_list("n4_t", n4)
         n5_t = load_list("n5_t", n5)
+        gn_t = sb.tile([P, PACK], F32, name="gn_t")
+        nc.sync.dma_start(gn_t[:], gn.rearrange("(p t) o -> p (t o)", t=PACK))
+        w_sc = load_scale_rows("w_sc", w1_scales, N, nc.sync)
         w_w = sb.tile([P, 2 * N], U8, name="w_w", align_bytes=64)
         nc.sync.dma_start(w_w[:].bitcast(I32), w1_words[0].bitcast(I32))
 
         def deal_bytes(dst, src):
             nc.vector.tensor_copy(dst.rearrange("p (t g i) -> p g t i", t=PACK, i=16), src.rearrange("p (g i t) -> p g t i", t=PACK, i=16))
 
-        def pick_scales(name, k_t, tok_t, extra, tag):
-            got = sb.tile([P, H + S], U8, name=name + "_got", tag=tag, align_bytes=64)
-            rows = sb.tile([P, H + S + extra], U8, name=name + "_rows", align_bytes=64)
-            nc.vector.tensor_copy(got[:, 0:H], d_sc[:].indirect(k_t[:]))
-            nc.vector.tensor_copy(got[:, H:], x_sc[:].indirect(tok_t[:]))
-            deal_bytes(rows[:, 0:H], got[:, 0:H])
-            nc.vector.tensor_copy(rows[:, H : H + S].bitcast(I32), got[:, H:].bitcast(I32))
+        def pick_scales(name, k_t, tok_t, x_tag, d_tag):
+            x_got = sb.tile([P, S], U8, name=name + "_xgot", tag=x_tag, align_bytes=64)
+            d_got = sb.tile([P, H], U8, name=name + "_dgot", tag=d_tag, align_bytes=64)
+            rows = sb.tile([P, H + S], U8, name=name + "_rows", align_bytes=64)
+            nc.vector.tensor_copy(x_got[:], x_sc[:].indirect(tok_t[:]))
+            nc.vector.tensor_copy(d_got[:], d_sc[:].indirect(k_t[:]))
+            deal_bytes(rows[:, 0:H], d_got[:])
+            nc.vector.tensor_copy(rows[:, H:].bitcast(I32), x_got[:].bitcast(I32))
             return rows
 
         def place_rows(name, rows, queue):
@@ -108,34 +109,41 @@ def tile_picked_twpqsoftbdot_none_po_kernel(
                 banks.append(bank)
             return banks
 
-        plane_b = place_rows("b", pick_scales("b", k2_t, two_t, 0, "b_got"), nc.scalar)
-        dealt_b, xw_b = pick_words("b", k2_t, two_t, "slot_y", "slot_x", "slot_z")
+        plane_b = place_rows("b", pick_scales("b", k2_t, two_t, "slot_y", "b_dgot"), nc.scalar)
+        dealt_b, xw_b = pick_words("b", k2_t, two_t, "slot_y", "slot_x", "b_dealt")
+        gain = sb.tile([P, PACK], F32, name="gain", tag="slot_g", align_bytes=64)
+        nc.gpsimd.tensor_scalar(gain[:], gn_t[:], 0.0625, 0.0, MULT, ADD)
         bank_b = product("acc_b", dealt_b, xw_b, plane_b)
         b_win = [sb.tile([P, 2 * S], F32, name="b_win" + str(t)) for t in range(PACK)]
         h_win = [sb.tile([P, 2 * S], F32, name="h_win" + str(t)) for t in range(PACK)]
         for t in range(PACK):
             nc.scalar.activation(b_win[t][:, S:], bank_b[t][:], TANH, scale=0.0625)
-            nc.scalar.activation(b_win[t][:, :S], bank_b[t][:], COPY, scale=gn_t[:, t : t + 1])
+            nc.scalar.activation(b_win[t][:, :S], bank_b[t][:], COPY, scale=gain[:, t : t + 1])
         for t in range(PACK):
             nc.scalar.activation(h_win[t][:, S:], b_win[t][:].indirect(n2_t[:]), COPY)
 
-        rows_a = pick_scales("a", k1_t, offs_t, N, "slot_x")
-        deal_bytes(rows_a[:, H + S :], w_sc[:])
-        plane_a = place_rows("a", rows_a, nc.sync)
-        dealt_a, xw_a = pick_words("a", k1_t, offs_t, "slot_z", "slot_y", "a_dealt")
+        plane_a = place_rows("a", pick_scales("a", k1_t, offs_t, "a_xgot", "slot_x"), nc.sync)
+        dealt_a, xw_a = pick_words("a", k1_t, offs_t, "d_sc", "slot_x", "a_dealt")
         bank_a = product("acc_a", dealt_a, xw_a, plane_a)
-        w_dealt = sb.tile([P, 2 * N], U8, name="w_dealt", tag="slot_y", align_bytes=64)
-        nc.vector.tensor_copy(
-            w_dealt[:].rearrange("p (t g i b) -> p g t i b", t=PACK, i=8, b=2), w_w[:].rearrange("p (g i t b) -> p g t i b", t=PACK, i=8, b=2)
-        )
+        w_cols = w_w[:].rearrange("p (g i t b) -> p g t i b", t=PACK, i=8, b=2)
+
+        def deal_w(pair, dst):
+            nc.vector.tensor_copy(dst.rearrange("p (t g i b) -> p g t i b", t=2, i=8, b=2), w_cols[:, :, 2 * pair : 2 * pair + 2])
+            return dst
+
+        w_first = sb.tile([P, 2 * N], U8, name="w_first", tag="slot_x", align_bytes=64)
+        deal_bytes(w_first[:, N:], w_sc[:])
+        plane_w = place_rows("w", w_first[:, N:], nc.sync)
+        w_dealt = [deal_w(0, w_first[:, :N])]
         a_win = [sb.tile([P, S], F32, name="a_win" + str(t)) for t in range(PACK)]
         for t in range(PACK):
-            nc.vector.tensor_scalar(a_win[t][:], bank_a[t][:], gn_t[:, t : t + 1], 0.0625, MULT, MULT)
-        prod = sb.tile([P, PACK, S], F32, name="prod", tag="slot_g")
+            nc.vector.tensor_scalar(a_win[t][:], bank_a[t][:], gain[:, t : t + 1], None, MULT)
+        w_second = sb.tile([P, N], U8, name="w_second", tag="slot_g", align_bytes=64)
+        w_dealt.append(deal_w(1, w_second[:]))
+        prod = sb.tile([P, PACK, S], F32, name="prod")
         for t in range(PACK):
-            nc.vector.scalar_tensor_tensor(prod[:, t, :], h_win[t][:, S:], 0.0625, b_win[t][:, S:], MULT, MULT)
+            nc.gpsimd.tensor_tensor(prod[:, t, :], h_win[t][:, S:], b_win[t][:, S:], MULT)
 
-        bank_h = [ps.tile([P, S], F32, name="acc_b" + str(t)) for t in range(PACK)]
         for u in range(2):
             cols = slice(u * HALF, (u + 1) * HALF)
             ents = slice(u * HALF // 16, (u + 1) * HALF // 16)
@@ -153,18 +161,20 @@ def tile_picked_twpqsoftbdot_none_po_kernel(
             z_sc = sb.tile([P, HALF], U8, name="z_sc" + str(u), align_bytes=64)
             nc.vector.quantize_mx(z_w[:].bitcast(FP8X4), z_sc[:], z_bf[:].rearrange("p c t -> p (c t)"))
             for t in range(PACK):
+                bank_h = ps.tile([P, HALF], F32, name=("acc_b", "acc_a")[u] + str(t))
                 nc.tensor.matmul_mx(
-                    bank_h[t][:, cols],
-                    lhsT=w_dealt[:, 2 * t * P : 2 * (t + 1) * P].bitcast(FP4X4),
-                    lhsT_scale=plane_a[:, H + S + t * P : H + S + (t + 1) * P],
+                    bank_h[:],
+                    lhsT=w_dealt[t // 2][:, 2 * (t % 2) * P : 2 * (t % 2 + 1) * P].bitcast(FP4X4),
+                    lhsT_scale=plane_w[:, t * P : (t + 1) * P],
                     rhs=z_w[:].bitcast(FP8X4),
                     rhs_scale=z_sc[:],
                     start=True,
                     stop=True,
                 )
-
-        for t in range(PACK):
-            nc.vector.tensor_copy(h_win[t][:, :S], bank_h[t][:])
+                if u == 0:
+                    nc.scalar.copy(h_win[t][:, cols], bank_h[:])
+                else:
+                    nc.vector.tensor_copy(h_win[t][:, cols], bank_h[:])
 
         y = sb.tile([P, PACK, S], F32, name="y")
         y_w = sb.tile([P, S], U32, name="y_w", align_bytes=64)
@@ -172,7 +182,7 @@ def tile_picked_twpqsoftbdot_none_po_kernel(
         out_rows = out_0.rearrange("(p t) j -> p t j", t=PACK)
         out_words = out_1[0].rearrange("p c r -> p (c r)").bitcast(I32)
 
-        def finish(t, lo, hi):
+        def finish(t, lo, hi, rounded):
             tag = str(t) + "_" + str(lo)
             ents = slice(lo // 16, hi // 16)
             got = [sb.tile([P, hi - lo], F32, name="got" + str(i) + "_" + tag) for i in range(3)]
@@ -182,16 +192,19 @@ def tile_picked_twpqsoftbdot_none_po_kernel(
             right = sb.tile([P, hi - lo], F32, name="right" + tag)
             nc.vector.scalar_tensor_tensor(left[:], h_win[t][:, lo:hi], 0.75, got[0][:], MULT, MULT)
             nc.vector.scalar_tensor_tensor(right[:], got[1][:], 0.75, got[2][:], MULT, MULT)
+            if rounded is not None:
+                nc.vector.tensor_tensor(rounded, left[:], right[:], ADD)
             nc.vector.tensor_tensor(y[:, t, lo:hi], left[:], right[:], ADD)
             nc.sync.dma_start(out_rows[:, t, lo:hi], y[:, t, lo:hi])
 
-        for t in range(PACK - 1):
-            finish(t, 0, S)
+        for t in range(2):
+            finish(t, 0, S, None)
         for u in range(2):
             lo, hi = u * HALF, (u + 1) * HALF
-            finish(PACK - 1, lo, hi)
             y_bf = sb.tile([P, HALF, PACK], BF16, name="y_bf" + str(u), align_bytes=64)
-            nc.vector.tensor_copy(y_bf[:].rearrange("p (c i) t -> p c t i", i=4), y[:, :, lo:hi].rearrange("p t (c i) -> p c t i", i=4))
+            nc.vector.tensor_copy(y_bf[:, :, :2].rearrange("p (c i) t -> p c t i", i=4), y[:, :2, lo:hi].rearrange("p t (c i) -> p c t i", i=4))
+            for t in range(2, PACK):
+                finish(t, lo, hi, y_bf[:, :, t])
             nc.vector.quantize_mx(y_w[:, lo:hi].bitcast(FP8X4), y_sc[:, lo:hi], y_bf[:].rearrange("p c t -> p (c t)"))
             nc.sync.dma_start(out_words[:, lo:hi], y_w[:, lo:hi].bitcast(I32))
         for q in range(4):

@@ -21,7 +21,22 @@ TANH = mybir.ActivationFunctionType.Tanh
 
 P = 128
 PACK = 4
+BLOCK_PARTS = 8
+QUAD = 32
+SCALE_ROWS = P // BLOCK_PARTS
+PER_COLUMN = 16
+LINE = 16
 HALF = S // 2
+ALIGN = 64
+AB_SCALE = 0.0625
+OUT_SCALE = 0.75
+
+DEAL_BUF = "deal_buf"
+B_TOKEN_BUF = "b_token_buf"
+D_SCALE_BUF = "d_sc"
+GAIN_BUF = "gain_buf"
+A_DEALT_BUF = "a_dealt"
+Z_BUF = "z_buf"
 
 
 def tile_picked_twpqsoftbdot_none_po_kernel(
@@ -38,21 +53,24 @@ def tile_picked_twpqsoftbdot_none_po_kernel(
             return tile
 
         def load_scale_rows(name, src, width, queue):
-            tile = sb.tile([P, width], U8, name=name, align_bytes=64)
-            queue.dma_start(tile[:].bitcast(I32), src[0].bitcast(I32).unsqueeze(1).to_broadcast([16, 8, width // 4]))
+            tile = sb.tile([P, width], U8, name=name, align_bytes=ALIGN)
+            queue.dma_start(tile[:].bitcast(I32), src[0].bitcast(I32).unsqueeze(1).to_broadcast([SCALE_ROWS, BLOCK_PARTS, width // 4]))
+            return tile
+
+        def load_words(name, src, width):
+            tile = sb.tile([P, width], U32, name=name, align_bytes=ALIGN)
+            nc.scalar.dma_start(tile[:].bitcast(I32), src[0].rearrange("p c r -> p (c r)").bitcast(I32))
             return tile
 
         two_t = load_list("two_t", two)
         x_sc = load_scale_rows("x_sc", x_scales, T, nc.scalar)
         k2_t = load_list("k2_t", k2)
-        d_sc = load_scale_rows("d_sc", d_scales, G, nc.scalar)
+        d_sc = load_scale_rows(D_SCALE_BUF, d_scales, G, nc.scalar)
         k1_t = load_list("k1_t", k1)
-        x_w = sb.tile([P, T], U32, name="x_w", align_bytes=64)
-        nc.scalar.dma_start(x_w[:].bitcast(I32), x_words[0].rearrange("p c r -> p (c r)").bitcast(I32))
+        x_w = load_words("x_w", x_words, T)
         n2_t = load_list("n2_t", n2)
         n1_t = load_list("n1_t", n1)
-        d_w = sb.tile([P, G], U32, name="d_w", align_bytes=64)
-        nc.scalar.dma_start(d_w[:].bitcast(I32), d_words[0].rearrange("p c r -> p (c r)").bitcast(I32))
+        d_w = load_words("d_w", d_words, G)
         offs_t = load_list("offs_t", offs)
         n3_t = load_list("n3_t", n3)
         n4_t = load_list("n4_t", n4)
@@ -60,36 +78,36 @@ def tile_picked_twpqsoftbdot_none_po_kernel(
         gn_t = sb.tile([P, PACK], F32, name="gn_t")
         nc.sync.dma_start(gn_t[:], gn.rearrange("(p t) o -> p (t o)", t=PACK))
         w_sc = load_scale_rows("w_sc", w1_scales, N, nc.sync)
-        w_w = sb.tile([P, 2 * N], U8, name="w_w", align_bytes=64)
+        w_w = sb.tile([P, 2 * N], U8, name="w_w", align_bytes=ALIGN)
         nc.sync.dma_start(w_w[:].bitcast(I32), w1_words[0].bitcast(I32))
 
-        def deal_bytes(dst, src):
-            nc.vector.tensor_copy(dst.rearrange("p (t g i) -> p g t i", t=PACK, i=16), src.rearrange("p (g i t) -> p g t i", t=PACK, i=16))
+        def deal(dst, src, run):
+            nc.vector.tensor_copy(dst.rearrange("p (t g i) -> p g t i", t=PACK, i=run), src.rearrange("p (g i t) -> p g t i", t=PACK, i=run))
 
         def pick_scales(name, k_t, tok_t, x_tag, d_tag):
-            x_got = sb.tile([P, S], U8, name=name + "_xgot", tag=x_tag, align_bytes=64)
-            d_got = sb.tile([P, H], U8, name=name + "_dgot", tag=d_tag, align_bytes=64)
-            rows = sb.tile([P, H + S], U8, name=name + "_rows", align_bytes=64)
+            x_got = sb.tile([P, S], U8, name=name + "_xgot", tag=x_tag, align_bytes=ALIGN)
+            d_got = sb.tile([P, H], U8, name=name + "_dgot", tag=d_tag, align_bytes=ALIGN)
+            rows = sb.tile([P, H + S], U8, name=name + "_rows", align_bytes=ALIGN)
             nc.vector.tensor_copy(x_got[:], x_sc[:].indirect(tok_t[:]))
             nc.vector.tensor_copy(d_got[:], d_sc[:].indirect(k_t[:]))
-            deal_bytes(rows[:, 0:H], d_got[:])
+            deal(rows[:, :H], d_got[:], LINE)
             nc.vector.tensor_copy(rows[:, H:].bitcast(I32), x_got[:].bitcast(I32))
             return rows
 
         def place_rows(name, rows, queue):
-            plane = sb.tile(list(rows.shape), U8, name=name + "_placed", align_bytes=64)
+            plane = sb.tile(list(rows.shape), U8, name=name + "_plane", align_bytes=ALIGN)
             nc.gpsimd.memset(plane[:].bitcast(I32), 0)
-            for q in range(4):
-                queue.dma_start(plane[32 * q : 32 * q + 4, :].bitcast(I32), rows[32 * q : 32 * q + 32 : 8, :].bitcast(I32))
+            for q in range(P // QUAD):
+                queue.dma_start(plane[QUAD * q : QUAD * q + PACK, :].bitcast(I32), rows[QUAD * q : QUAD * (q + 1) : BLOCK_PARTS, :].bitcast(I32))
             return plane
 
-        def pick_words(name, k_t, tok_t, x_tag, d_tag, dealt_tag):
-            x_got = sb.tile([P, S], U32, name=name + "_xw", tag=x_tag, align_bytes=64)
-            d_got = sb.tile([P, H], U32, name=name + "_dw", tag=d_tag, align_bytes=64)
-            dealt = sb.tile([P, H], U32, name=name + "_dealt", tag=dealt_tag, align_bytes=64)
+        def pick_words(name, k_t, tok_t, x_tag, dealt_tag):
+            x_got = sb.tile([P, S], U32, name=name + "_xw", tag=x_tag, align_bytes=ALIGN)
+            d_got = sb.tile([P, H], U32, name=name + "_dw", tag=DEAL_BUF, align_bytes=ALIGN)
+            dealt = sb.tile([P, H], U32, name=name + "_dealt", tag=dealt_tag, align_bytes=ALIGN)
             nc.vector.tensor_copy(d_got[:], d_w[:].indirect(k_t[:]))
             nc.vector.tensor_copy(x_got[:], x_w[:].indirect(tok_t[:]))
-            nc.vector.tensor_copy(dealt[:].rearrange("p (t g i) -> p g t i", t=PACK, i=4), d_got[:].rearrange("p (g i t) -> p g t i", t=PACK, i=4))
+            deal(dealt[:], d_got[:], LINE // 4)
             return dealt, x_got
 
         def product(bank_name, dealt, x_got, plane):
@@ -102,43 +120,50 @@ def tile_picked_twpqsoftbdot_none_po_kernel(
                     lhsT=dealt[:, cols].bitcast(FP8X4),
                     lhsT_scale=plane[:, cols],
                     rhs=x_got[:].bitcast(FP8X4),
-                    rhs_scale=plane[:, H : H + S],
+                    rhs_scale=plane[:, H:],
                     start=True,
                     stop=True,
                 )
                 banks.append(bank)
             return banks
 
-        plane_b = place_rows("b", pick_scales("b", k2_t, two_t, "slot_y", "b_dgot"), nc.scalar)
-        dealt_b, xw_b = pick_words("b", k2_t, two_t, "slot_y", "slot_x", "b_dealt")
-        gain = sb.tile([P, PACK], F32, name="gain", tag="slot_g", align_bytes=64)
-        nc.gpsimd.tensor_scalar(gain[:], gn_t[:], 0.0625, 0.0, MULT, ADD)
+        def by_fours(tiles):
+            return tiles.rearrange("p t (c i) -> p c t i", i=LINE // 4)
+
+        def interleaved(rounded):
+            return rounded.rearrange("p (c i) t -> p c t i", i=LINE // 4)
+
+        plane_b = place_rows("b", pick_scales("b", k2_t, two_t, B_TOKEN_BUF, "b_dgot"), nc.scalar)
+        dealt_b, xw_b = pick_words("b", k2_t, two_t, B_TOKEN_BUF, "b_dealt")
+        gain = sb.tile([P, PACK], F32, name="gain", tag=GAIN_BUF, align_bytes=ALIGN)
+        nc.gpsimd.tensor_scalar(gain[:], gn_t[:], AB_SCALE, 0.0, MULT, ADD)
         bank_b = product("acc_b", dealt_b, xw_b, plane_b)
         b_win = [sb.tile([P, 2 * S], F32, name="b_win" + str(t)) for t in range(PACK)]
         h_win = [sb.tile([P, 2 * S], F32, name="h_win" + str(t)) for t in range(PACK)]
         for t in range(PACK):
-            nc.scalar.activation(b_win[t][:, S:], bank_b[t][:], TANH, scale=0.0625)
+            nc.scalar.activation(b_win[t][:, S:], bank_b[t][:], TANH, scale=AB_SCALE)
             nc.scalar.activation(b_win[t][:, :S], bank_b[t][:], COPY, scale=gain[:, t : t + 1])
         for t in range(PACK):
             nc.scalar.activation(h_win[t][:, S:], b_win[t][:].indirect(n2_t[:]), COPY)
 
-        plane_a = place_rows("a", pick_scales("a", k1_t, offs_t, "a_xgot", "slot_x"), nc.sync)
-        dealt_a, xw_a = pick_words("a", k1_t, offs_t, "d_sc", "slot_x", "a_dealt")
+        plane_a = place_rows("a", pick_scales("a", k1_t, offs_t, "a_xgot", DEAL_BUF), nc.sync)
+        dealt_a, xw_a = pick_words("a", k1_t, offs_t, D_SCALE_BUF, A_DEALT_BUF)
         bank_a = product("acc_a", dealt_a, xw_a, plane_a)
-        w_cols = w_w[:].rearrange("p (g i t b) -> p g t i b", t=PACK, i=8, b=2)
+
+        w_cols = w_w[:].rearrange("p (g i t b) -> p g t i b", t=PACK, i=LINE // 2, b=2)
 
         def deal_w(pair, dst):
-            nc.vector.tensor_copy(dst.rearrange("p (t g i b) -> p g t i b", t=2, i=8, b=2), w_cols[:, :, 2 * pair : 2 * pair + 2])
+            nc.vector.tensor_copy(dst.rearrange("p (t g i b) -> p g t i b", t=2, i=LINE // 2, b=2), w_cols[:, :, 2 * pair : 2 * pair + 2])
             return dst
 
-        w_first = sb.tile([P, 2 * N], U8, name="w_first", tag="slot_x", align_bytes=64)
-        deal_bytes(w_first[:, N:], w_sc[:])
+        w_first = sb.tile([P, 2 * N], U8, name="w_first", tag=DEAL_BUF, align_bytes=ALIGN)
+        deal(w_first[:, N:], w_sc[:], LINE)
         plane_w = place_rows("w", w_first[:, N:], nc.sync)
         w_dealt = [deal_w(0, w_first[:, :N])]
         a_win = [sb.tile([P, S], F32, name="a_win" + str(t)) for t in range(PACK)]
         for t in range(PACK):
             nc.vector.tensor_scalar(a_win[t][:], bank_a[t][:], gain[:, t : t + 1], None, MULT)
-        w_second = sb.tile([P, N], U8, name="w_second", tag="slot_g", align_bytes=64)
+        w_second = sb.tile([P, N], U8, name="w_second", tag=A_DEALT_BUF, align_bytes=ALIGN)
         w_dealt.append(deal_w(1, w_second[:]))
         prod = sb.tile([P, PACK, S], F32, name="prod")
         for t in range(PACK):
@@ -146,19 +171,14 @@ def tile_picked_twpqsoftbdot_none_po_kernel(
 
         for u in range(2):
             cols = slice(u * HALF, (u + 1) * HALF)
-            ents = slice(u * HALF // 16, (u + 1) * HALF // 16)
-            a_got = sb.tile([P, PACK, HALF], F32, name="a_got" + str(u))
+            ents = slice(u * HALF // PER_COLUMN, (u + 1) * HALF // PER_COLUMN)
+            a_got = sb.tile([P, PACK, HALF], F32, name="a_got" + str(u), tag=("a_got", GAIN_BUF)[u], align_bytes=ALIGN)
             for t in range(PACK):
                 nc.scalar.activation(a_got[:, t, :], a_win[t][:].indirect(n1_t[:, ents]), COPY)
-            z_bf = sb.tile([P, HALF, PACK], BF16, name="z_bf" + str(u), align_bytes=64)
-            nc.vector.tensor_tensor(
-                z_bf[:].rearrange("p (c i) t -> p c t i", i=4),
-                a_got[:].rearrange("p t (c i) -> p c t i", i=4),
-                prod[:, :, cols].rearrange("p t (c i) -> p c t i", i=4),
-                SUB,
-            )
-            z_w = sb.tile([P, HALF], U32, name="z_w" + str(u), align_bytes=64)
-            z_sc = sb.tile([P, HALF], U8, name="z_sc" + str(u), align_bytes=64)
+            z_bf = sb.tile([P, HALF, PACK], BF16, name="z_bf" + str(u), tag=Z_BUF, align_bytes=ALIGN)
+            nc.vector.tensor_tensor(interleaved(z_bf[:]), by_fours(a_got[:]), by_fours(prod[:, :, cols]), SUB)
+            z_w = sb.tile([P, HALF], U32, name="z_w" + str(u), align_bytes=ALIGN)
+            z_sc = sb.tile([P, HALF], U8, name="z_sc" + str(u), align_bytes=ALIGN)
             nc.vector.quantize_mx(z_w[:].bitcast(FP8X4), z_sc[:], z_bf[:].rearrange("p c t -> p (c t)"))
             for t in range(PACK):
                 bank_h = ps.tile([P, HALF], F32, name=("acc_b", "acc_a")[u] + str(t))
@@ -171,42 +191,42 @@ def tile_picked_twpqsoftbdot_none_po_kernel(
                     start=True,
                     stop=True,
                 )
-                if u == 0:
-                    nc.scalar.copy(h_win[t][:, cols], bank_h[:])
-                else:
-                    nc.vector.tensor_copy(h_win[t][:, cols], bank_h[:])
+                (nc.scalar.copy, nc.vector.tensor_copy)[u](h_win[t][:, cols], bank_h[:])
 
         y = sb.tile([P, PACK, S], F32, name="y")
-        y_w = sb.tile([P, S], U32, name="y_w", align_bytes=64)
-        y_sc = sb.tile([P, S], U8, name="y_sc", align_bytes=64)
+        y_w = sb.tile([P, S], U32, name="y_w", align_bytes=ALIGN)
+        y_sc = sb.tile([P, S], U8, name="y_sc", align_bytes=ALIGN)
         out_rows = out_0.rearrange("(p t) j -> p t j", t=PACK)
         out_words = out_1[0].rearrange("p c r -> p (c r)").bitcast(I32)
 
-        def finish(t, lo, hi, rounded):
-            tag = str(t) + "_" + str(lo)
-            ents = slice(lo // 16, hi // 16)
-            got = [sb.tile([P, hi - lo], F32, name="got" + str(i) + "_" + tag) for i in range(3)]
+        def terms(t, lo, hi):
+            suffix = str(t) + "_" + str(lo)
+            ents = slice(lo // PER_COLUMN, hi // PER_COLUMN)
+            got = [sb.tile([P, hi - lo], F32, name="got" + str(i) + "_" + suffix) for i in range(3)]
             for i, lst in enumerate((n3_t, n4_t, n5_t)):
                 nc.scalar.activation(got[i][:], h_win[t][:].indirect(lst[:, ents]), COPY)
-            left = sb.tile([P, hi - lo], F32, name="left" + tag)
-            right = sb.tile([P, hi - lo], F32, name="right" + tag)
-            nc.vector.scalar_tensor_tensor(left[:], h_win[t][:, lo:hi], 0.75, got[0][:], MULT, MULT)
-            nc.vector.scalar_tensor_tensor(right[:], got[1][:], 0.75, got[2][:], MULT, MULT)
-            if rounded is not None:
-                nc.vector.tensor_tensor(rounded, left[:], right[:], ADD)
+            left = sb.tile([P, hi - lo], F32, name="left" + suffix)
+            right = sb.tile([P, hi - lo], F32, name="right" + suffix)
+            nc.vector.scalar_tensor_tensor(left[:], h_win[t][:, lo:hi], OUT_SCALE, got[0][:], MULT, MULT)
+            nc.vector.scalar_tensor_tensor(right[:], got[1][:], OUT_SCALE, got[2][:], MULT, MULT)
+            return left, right
+
+        def add_and_store(t, lo, hi, left, right):
             nc.vector.tensor_tensor(y[:, t, lo:hi], left[:], right[:], ADD)
             nc.sync.dma_start(out_rows[:, t, lo:hi], y[:, t, lo:hi])
 
         for t in range(2):
-            finish(t, 0, S, None)
+            add_and_store(t, 0, S, *terms(t, 0, S))
         for u in range(2):
             lo, hi = u * HALF, (u + 1) * HALF
-            y_bf = sb.tile([P, HALF, PACK], BF16, name="y_bf" + str(u), align_bytes=64)
-            nc.vector.tensor_copy(y_bf[:, :, :2].rearrange("p (c i) t -> p c t i", i=4), y[:, :2, lo:hi].rearrange("p t (c i) -> p c t i", i=4))
+            y_bf = sb.tile([P, HALF, PACK], BF16, name="y_bf" + str(u), align_bytes=ALIGN)
+            nc.vector.tensor_copy(interleaved(y_bf[:, :, :2]), by_fours(y[:, :2, lo:hi]))
             for t in range(2, PACK):
-                finish(t, lo, hi, y_bf[:, :, t])
+                left, right = terms(t, lo, hi)
+                nc.vector.tensor_tensor(y_bf[:, :, t], left[:], right[:], ADD)
+                add_and_store(t, lo, hi, left, right)
             nc.vector.quantize_mx(y_w[:, lo:hi].bitcast(FP8X4), y_sc[:, lo:hi], y_bf[:].rearrange("p c t -> p (c t)"))
             nc.sync.dma_start(out_words[:, lo:hi], y_w[:, lo:hi].bitcast(I32))
-        for q in range(4):
-            queue = nc.scalar if q % 2 == 0 else nc.sync
-            queue.dma_start(out_2[0, 4 * q : 4 * q + 4, :].bitcast(I32), y_sc[32 * q : 32 * q + 4, :].bitcast(I32))
+        for q in range(P // QUAD):
+            queue = (nc.scalar, nc.sync)[q % 2]
+            queue.dma_start(out_2[0, PACK * q : PACK * (q + 1), :].bitcast(I32), y_sc[QUAD * q : QUAD * q + PACK, :].bitcast(I32))

from contextlib import ExitStack

import concourse.mybir as mybir

K, T, S, N, G, H = 512, 1024, 256, 512, 2048, 512
FLOPS = 2 * K * H * S * 2 + 2 * H * N * S

F32 = mybir.dt.float32
BF16 = mybir.dt.bfloat16
I32 = mybir.dt.int32
U32 = mybir.dt.uint32
U16 = mybir.dt.uint16
U8 = mybir.dt.uint8
FP8X4 = mybir.dt.float8_e4m3fn_x4
FP4X4 = mybir.dt.float4_e2m1fn_x4
MULT = mybir.AluOpType.mult
ADD = mybir.AluOpType.add
SUB = mybir.AluOpType.subtract
COPY = mybir.ActivationFunctionType.Copy
TANH = mybir.ActivationFunctionType.Tanh

P = 128
PACK = 4
BLOCK_PARTS = 8
QUAD = 32
SCALE_ROWS = P // BLOCK_PARTS
PER_COLUMN = 16
LINE = 16
HALF = S // 2
ALIGN = 64
AB_SCALE = 0.0625
OUT_SCALE = 0.75

DEAL_BUF = "deal_buf"
B_TOKEN_BUF = "b_token_buf"
D_SCALE_BUF = "d_sc"
GAIN_BUF = "gain_buf"
A_DEALT_BUF = "a_dealt"
Z_BUF = "z_buf"


def tile_picked_twpqsoftbdot_none_po_kernel(
    tc, x_words, x_scales, d_words, d_scales, gn, w1_words, w1_scales, offs, k1, two, k2, n1, n2, n3, n4, n5, out_0, out_1, out_2
):
    nc = tc.nc
    with ExitStack() as ctx:
        sb = ctx.enter_context(tc.tile_pool(name="sb", bufs=1))
        ps = ctx.enter_context(tc.psum_pool(name="ps", bufs=1))

        def load_list(name, src):
            tile = sb.tile(list(src.shape), U16, name=name)
            nc.sync.dma_start(tile[:], src)
            return tile

        def load_scale_rows(name, src, width, queue):
            tile = sb.tile([P, width], U8, name=name, align_bytes=ALIGN)
            queue.dma_start(tile[:].bitcast(I32), src[0].bitcast(I32).unsqueeze(1).to_broadcast([SCALE_ROWS, BLOCK_PARTS, width // 4]))
            return tile

        def load_words(name, src, width):
            tile = sb.tile([P, width], U32, name=name, align_bytes=ALIGN)
            nc.scalar.dma_start(tile[:].bitcast(I32), src[0].rearrange("p c r -> p (c r)").bitcast(I32))
            return tile

        two_t = load_list("two_t", two)
        x_sc = load_scale_rows("x_sc", x_scales, T, nc.scalar)
        k2_t = load_list("k2_t", k2)
        d_sc = load_scale_rows(D_SCALE_BUF, d_scales, G, nc.scalar)
        k1_t = load_list("k1_t", k1)
        x_w = load_words("x_w", x_words, T)
        n2_t = load_list("n2_t", n2)
        n1_t = load_list("n1_t", n1)
        d_w = load_words("d_w", d_words, G)
        offs_t = load_list("offs_t", offs)
        n3_t = load_list("n3_t", n3)
        n4_t = load_list("n4_t", n4)
        n5_t = load_list("n5_t", n5)
        gn_t = sb.tile([P, PACK], F32, name="gn_t")
        nc.sync.dma_start(gn_t[:], gn.rearrange("(p t) o -> p (t o)", t=PACK))
        w_sc = load_scale_rows("w_sc", w1_scales, N, nc.sync)
        w_w = sb.tile([P, 2 * N], U8, name="w_w", align_bytes=ALIGN)
        nc.sync.dma_start(w_w[:].bitcast(I32), w1_words[0].bitcast(I32))

        def deal(dst, src, run):
            nc.vector.tensor_copy(dst.rearrange("p (t g i) -> p g t i", t=PACK, i=run), src.rearrange("p (g i t) -> p g t i", t=PACK, i=run))

        def pick_scales(name, k_t, tok_t, x_tag, d_tag):
            x_got = sb.tile([P, S], U8, name=name + "_xgot", tag=x_tag, align_bytes=ALIGN)
            d_got = sb.tile([P, H], U8, name=name + "_dgot", tag=d_tag, align_bytes=ALIGN)
            rows = sb.tile([P, H + S], U8, name=name + "_rows", align_bytes=ALIGN)
            nc.vector.tensor_copy(x_got[:], x_sc[:].indirect(tok_t[:]))
            nc.vector.tensor_copy(d_got[:], d_sc[:].indirect(k_t[:]))
            deal(rows[:, :H], d_got[:], LINE)
            nc.vector.tensor_copy(rows[:, H:].bitcast(I32), x_got[:].bitcast(I32))
            return rows

        def place_rows(name, rows, queue):
            plane = sb.tile(list(rows.shape), U8, name=name + "_plane", align_bytes=ALIGN)
            nc.gpsimd.memset(plane[:].bitcast(I32), 0)
            for q in range(P // QUAD):
                queue.dma_start(plane[QUAD * q : QUAD * q + PACK, :].bitcast(I32), rows[QUAD * q : QUAD * (q + 1) : BLOCK_PARTS, :].bitcast(I32))
            return plane

        def pick_words(name, k_t, tok_t, x_tag, dealt_tag):
            x_got = sb.tile([P, S], U32, name=name + "_xw", tag=x_tag, align_bytes=ALIGN)
            d_got = sb.tile([P, H], U32, name=name + "_dw", tag=DEAL_BUF, align_bytes=ALIGN)
            dealt = sb.tile([P, H], U32, name=name + "_dealt", tag=dealt_tag, align_bytes=ALIGN)
            nc.vector.tensor_copy(d_got[:], d_w[:].indirect(k_t[:]))
            nc.vector.tensor_copy(x_got[:], x_w[:].indirect(tok_t[:]))
            deal(dealt[:], d_got[:], LINE // 4)
            return dealt, x_got

        def product(bank_name, dealt, x_got, plane):
            banks = []
            for t in range(PACK):
                bank = ps.tile([P, S], F32, name=bank_name + str(t))
                cols = slice(t * P, (t + 1) * P)
                nc.tensor.matmul_mx(
                    bank[:],
                    lhsT=dealt[:, cols].bitcast(FP8X4),
                    lhsT_scale=plane[:, cols],
                    rhs=x_got[:].bitcast(FP8X4),
                    rhs_scale=plane[:, H:],
                    start=True,
                    stop=True,
                )
                banks.append(bank)
            return banks

        def by_fours(tiles):
            return tiles.rearrange("p t (c i) -> p c t i", i=LINE // 4)

        def interleaved(rounded):
            return rounded.rearrange("p (c i) t -> p c t i", i=LINE // 4)

        plane_b = place_rows("b", pick_scales("b", k2_t, two_t, B_TOKEN_BUF, "b_dgot"), nc.scalar)
        dealt_b, xw_b = pick_words("b", k2_t, two_t, B_TOKEN_BUF, "b_dealt")
        gain = sb.tile([P, PACK], F32, name="gain", tag=GAIN_BUF, align_bytes=ALIGN)
        nc.gpsimd.tensor_scalar(gain[:], gn_t[:], AB_SCALE, 0.0, MULT, ADD)
        bank_b = product("acc_b", dealt_b, xw_b, plane_b)
        b_win = [sb.tile([P, 2 * S], F32, name="b_win" + str(t)) for t in range(PACK)]
        h_win = [sb.tile([P, 2 * S], F32, name="h_win" + str(t)) for t in range(PACK)]
        for t in range(PACK):
            nc.scalar.activation(b_win[t][:, S:], bank_b[t][:], TANH, scale=AB_SCALE)
            nc.scalar.activation(b_win[t][:, :S], bank_b[t][:], COPY, scale=gain[:, t : t + 1])
        for t in range(PACK):
            nc.scalar.activation(h_win[t][:, S:], b_win[t][:].indirect(n2_t[:]), COPY)

        plane_a = place_rows("a", pick_scales("a", k1_t, offs_t, "a_xgot", DEAL_BUF), nc.sync)
        dealt_a, xw_a = pick_words("a", k1_t, offs_t, D_SCALE_BUF, A_DEALT_BUF)
        bank_a = product("acc_a", dealt_a, xw_a, plane_a)

        w_cols = w_w[:].rearrange("p (g i t b) -> p g t i b", t=PACK, i=LINE // 2, b=2)

        def deal_w(pair, dst):
            nc.vector.tensor_copy(dst.rearrange("p (t g i b) -> p g t i b", t=2, i=LINE // 2, b=2), w_cols[:, :, 2 * pair : 2 * pair + 2])
            return dst

        w_first = sb.tile([P, 2 * N], U8, name="w_first", tag=DEAL_BUF, align_bytes=ALIGN)
        deal(w_first[:, N:], w_sc[:], LINE)
        plane_w = place_rows("w", w_first[:, N:], nc.sync)
        w_dealt = [deal_w(0, w_first[:, :N])]
        a_win = [sb.tile([P, S], F32, name="a_win" + str(t)) for t in range(PACK)]
        for t in range(PACK):
            nc.vector.tensor_scalar(a_win[t][:], bank_a[t][:], gain[:, t : t + 1], None, MULT)
        w_second = sb.tile([P, N], U8, name="w_second", tag=A_DEALT_BUF, align_bytes=ALIGN)
        w_dealt.append(deal_w(1, w_second[:]))
        prod = sb.tile([P, PACK, S], F32, name="prod")
        for t in range(PACK):
            nc.gpsimd.tensor_tensor(prod[:, t, :], h_win[t][:, S:], b_win[t][:, S:], MULT)

        for u in range(2):
            cols = slice(u * HALF, (u + 1) * HALF)
            ents = slice(u * HALF // PER_COLUMN, (u + 1) * HALF // PER_COLUMN)
            a_got = sb.tile([P, PACK, HALF], F32, name="a_got" + str(u), tag=("a_got", GAIN_BUF)[u], align_bytes=ALIGN)
            for t in range(PACK):
                nc.scalar.activation(a_got[:, t, :], a_win[t][:].indirect(n1_t[:, ents]), COPY)
            z_bf = sb.tile([P, HALF, PACK], BF16, name="z_bf" + str(u), tag=Z_BUF, align_bytes=ALIGN)
            nc.vector.tensor_tensor(interleaved(z_bf[:]), by_fours(a_got[:]), by_fours(prod[:, :, cols]), SUB)
            z_w = sb.tile([P, HALF], U32, name="z_w" + str(u), align_bytes=ALIGN)
            z_sc = sb.tile([P, HALF], U8, name="z_sc" + str(u), align_bytes=ALIGN)
            nc.vector.quantize_mx(z_w[:].bitcast(FP8X4), z_sc[:], z_bf[:].rearrange("p c t -> p (c t)"))
            for t in range(PACK):
                bank_h = ps.tile([P, HALF], F32, name=("acc_b", "acc_a")[u] + str(t))
                nc.tensor.matmul_mx(
                    bank_h[:],
                    lhsT=w_dealt[t // 2][:, 2 * (t % 2) * P : 2 * (t % 2 + 1) * P].bitcast(FP4X4),
                    lhsT_scale=plane_w[:, t * P : (t + 1) * P],
                    rhs=z_w[:].bitcast(FP8X4),
                    rhs_scale=z_sc[:],
                    start=True,
                    stop=True,
                )
                (nc.scalar.copy, nc.vector.tensor_copy)[u](h_win[t][:, cols], bank_h[:])

        y = sb.tile([P, PACK, S], F32, name="y")
        y_w = sb.tile([P, S], U32, name="y_w", align_bytes=ALIGN)
        y_sc = sb.tile([P, S], U8, name="y_sc", align_bytes=ALIGN)
        out_rows = out_0.rearrange("(p t) j -> p t j", t=PACK)
        out_words = out_1[0].rearrange("p c r -> p (c r)").bitcast(I32)

        def terms(t, lo, hi):
            suffix = str(t) + "_" + str(lo)
            ents = slice(lo // PER_COLUMN, hi // PER_COLUMN)
            got = [sb.tile([P, hi - lo], F32, name="got" + str(i) + "_" + suffix) for i in range(3)]
            for i, lst in enumerate((n3_t, n4_t, n5_t)):
                nc.scalar.activation(got[i][:], h_win[t][:].indirect(lst[:, ents]), COPY)
            left = sb.tile([P, hi - lo], F32, name="left" + suffix)
            right = sb.tile([P, hi - lo], F32, name="right" + suffix)
            nc.vector.scalar_tensor_tensor(left[:], h_win[t][:, lo:hi], OUT_SCALE, got[0][:], MULT, MULT)
            nc.vector.scalar_tensor_tensor(right[:], got[1][:], OUT_SCALE, got[2][:], MULT, MULT)
            return left, right

        def add_and_store(t, lo, hi, left, right):
            nc.vector.tensor_tensor(y[:, t, lo:hi], left[:], right[:], ADD)
            nc.sync.dma_start(out_rows[:, t, lo:hi], y[:, t, lo:hi])

        for t in range(2):
            add_and_store(t, 0, S, *terms(t, 0, S))
        for u in range(2):
            lo, hi = u * HALF, (u + 1) * HALF
            y_bf = sb.tile([P, HALF, PACK], BF16, name="y_bf" + str(u), align_bytes=ALIGN)
            nc.vector.tensor_copy(interleaved(y_bf[:, :, :2]), by_fours(y[:, :2, lo:hi]))
            for t in range(2, PACK):
                left, right = terms(t, lo, hi)
                nc.vector.tensor_tensor(y_bf[:, :, t], left[:], right[:], ADD)
                add_and_store(t, lo, hi, left, right)
            nc.vector.quantize_mx(y_w[:, lo:hi].bitcast(FP8X4), y_sc[:, lo:hi], y_bf[:].rearrange("p c t -> p (c t)"))
            nc.sync.dma_start(out_words[:, lo:hi], y_w[:, lo:hi].bitcast(I32))
        for q in range(P // QUAD):
            queue = (nc.scalar, nc.sync)[q % 2]
            queue.dma_start(out_2[0, PACK * q : PACK * (q + 1), :].bitcast(I32), y_sc[QUAD * q : QUAD * q + PACK, :].bitcast(I32))
